import numpy as np
import ml_dtypes


def mxq(x, axis, fmt="e4m3"):
    dtype, down = {"e4m3": (ml_dtypes.float8_e4m3fn, 7), "e5m2": (ml_dtypes.float8_e5m2, 14)}[fmt]
    v = np.moveaxis(np.asarray(x, np.float32).astype(ml_dtypes.bfloat16).astype(np.float64), axis, -1)
    blocks = v.reshape(v.shape[:-1] + (-1, 32))
    amax = np.abs(blocks).max(-1, keepdims=True)
    byte = np.maximum(np.where(amax > 0, np.frexp(amax)[1] - 1 + 127, 0) - down, 1)
    scale = np.exp2(byte - 127.0)
    codes = (blocks / scale).astype(np.float32).astype(dtype).astype(np.float64)
    return np.moveaxis((codes * scale).reshape(v.shape), -1, axis)


WIDE = False


def mx_kscale(k):
    if not WIDE:
        return np.ones(k)
    levels = np.array([30, -30])
    if k % 512:
        return np.exp2(np.random.permutation(np.resize(levels, k // 32))).repeat(32)
    a = np.empty((k // 512, 16))
    for p in range(k // 512):
        a[p, :8] = np.random.permutation(np.resize(levels, 8))
        for g in range(8):
            far = levels[np.abs(levels - a[p, g]) >= 10]
            a[p, g + 8] = far[np.random.randint(len(far))]
    return np.exp2(a.ravel()).repeat(32)


BF16 = ml_dtypes.bfloat16


def bf(x):
    return np.asarray(x, np.float32).astype(BF16)


def f64(x):
    return np.asarray(x).astype(np.float64)


E2M1 = np.array([0.0, 0.5, 1.0, 1.5, 2.0, 3.0, 4.0, 6.0, -0.0, -0.5, -1.0, -1.5, -2.0, -3.0, -4.0, -6.0])


def pack_weight(w, fmt):
    k, n = w.shape
    w = f64(bf(w)).reshape(k // 32, 32, n)
    amax = np.abs(w).max(1)
    if fmt == "e4m3":
        byte = np.frexp(amax)[1] - 1 + 127 - 7
    else:
        mant, ex = np.frexp(amax / 6.0)
        byte = np.where(mant > 0.5, ex, ex - 1) + 127
    byte = np.clip(np.where(amax > 0, byte, 1), 1, 254)
    scaled = (w * np.exp2(127.0 - byte)[:, None, :]).reshape(k, n).astype(np.float32)
    by_word = np.ascontiguousarray(scaled.reshape(k // 512, 128, 4, n).transpose(0, 1, 3, 2))
    if fmt == "e4m3":
        words = by_word.astype(ml_dtypes.float8_e4m3fn).view(np.uint8)
    else:
        c = by_word.astype(ml_dtypes.float4_e2m1fn).view(np.uint8) & 0xF
        words = c[..., 0::2] | (c[..., 1::2] << 4)
    return np.ascontiguousarray(words), np.ascontiguousarray(byte.astype(np.uint8).reshape(k // 512, 16, n))


def unpack_weight(words, scales, fmt):
    g, p, n, _ = words.shape
    if fmt == "e4m3":
        vals = np.ascontiguousarray(words).view(ml_dtypes.float8_e4m3fn).astype(np.float64)
    else:
        nib = np.empty((g, p, n, 4), np.uint8)
        nib[..., 0::2] = words & 0xF
        nib[..., 1::2] = words >> 4
        vals = E2M1[nib]
    vals = vals * np.repeat(np.exp2(scales.astype(np.float64) - 127.0), 8, axis=1)[..., None]
    return vals.transpose(0, 1, 3, 2).reshape(g * 512, n)
def pack4(w):
    words, scales = pack_weight(w, "e2m1")
    return words.reshape(words.shape[0], 128, -1), scales


def unpack4(words, scales):
    return unpack_weight(words.reshape(words.shape[0], 128, -1, 2), scales, "e2m1")


M, K, L, N = 1024, 1024, 1024, 3072


def setup_inputs():
    s, t = mx_kscale(K), mx_kscale(L)
    words, scales = pack4(np.random.standard_normal((K, L)) / np.sqrt(K) / s[:, None] * t)
    return {"pilots": bf(np.random.standard_normal((M, K)) * s),
            "to_taps_words": words,
            "to_taps_scales": scales,
            "pdp": bf(np.exp(-3.0 * np.random.random(L))),
            "noise": bf(0.1 + 0.5 * np.random.random(M)),
            "to_sub": bf(np.random.standard_normal((L, N)) / np.sqrt(L) / t[:, None]),
            "front_end": bf(1 + 0.1 * np.random.standard_normal(N))}


def reference(pilots, to_taps_words, to_taps_scales, pdp, noise, to_sub, front_end):
    w = unpack4(to_taps_words, to_taps_scales)
    taps = mxq(f64(pilots), 1, "e4m3") @ w
    power = f64(pdp)
    shrink = power / (power + f64(noise)[:, None])
    clean = taps * shrink
    sub = mxq(clean, 1, "e5m2") @ mxq(f64(to_sub), 0, "e4m3")
    return sub * f64(front_end)

@@ -1,0 +1,330 @@
+from contextlib import ExitStack
+
+import concourse.mybir as mybir
+from concourse.masks import make_identity
+
+M, K, L, N = 1024, 1024, 1024, 3072
+FLOPS = 2 * M * K * L + 2 * M * L * N
+
+F32 = mybir.dt.float32
+BF16 = mybir.dt.bfloat16
+I32 = mybir.dt.int32
+U32 = mybir.dt.uint32
+U8 = mybir.dt.uint8
+E4M3 = mybir.dt.float8_e4m3fn_x4
+E5M2 = mybir.dt.float8_e5m2_x4
+E2M1 = mybir.dt.float4_e2m1fn_x4
+ALU = mybir.AluOpType
+ACT = mybir.ActivationFunctionType
+
+P = 128
+PACK = 4
+PASSES = 2
+TILES = M // P
+BANK = 512
+STRIPS = N // BANK
+LN_EDGE = 2.0 ** 64
+SHARED_A = (1, 3, 5, 6)
+SHARED_B = (0, 1, 2, 4, 5)
+
+
+def tile_delay_domain_denoising_s9_kernel(tc, pilots, to_taps_words, to_taps_scales, pdp, noise, to_sub, front_end, out):
+    nc = tc.nc
+    pilot_rows = pilots.rearrange("(p i) k -> p i k", i=TILES)
+    out_rows = out.rearrange("(p i) n -> p i n", i=TILES)
+    sub_rows = to_sub.rearrange("(g p t) n -> g p t n", g=PASSES, t=PACK)
+
+    with ExitStack() as ctx:
+        keep = ctx.enter_context(tc.tile_pool(name="keep", bufs=1))
+        work = ctx.enter_context(tc.tile_pool(name="work", bufs=3))
+        psum = ctx.enter_context(tc.psum_pool(name="psum", bufs=1))
+        ctx.enter_context(tc.manual_schedule())
+
+        banks_taken = []
+
+        def next_bank():
+            tag = "bank%d" % (len(banks_taken) % 8)
+            banks_taken.append(tag)
+            return psum.tile([P, BANK], F32, name=tag, tag=tag)
+
+        w_scales = keep.tile([P, PASSES, L], U8, name="w_scales", align_bytes=64)
+        nc.vector.memset(w_scales[:].rearrange("p g n -> p (g n)").bitcast(I32), 0)
+        one = keep.tile([P, 1], F32, name="one")
+        nc.vector.memset(one[:], 1.0)
+        warm = keep.tile([P, 2], F32, name="warm")
+        nc.scalar.activation(out=warm[:, 0:1], in_=one[:], func=ACT.Ln)
+        ident = keep.tile([P, P], F32, name="ident")
+        make_identity(nc, ident[:])
+
+        powers = keep.tile([P, 2, 16], BF16, name="powers")
+        nc.sync.dma_start(out=powers[:, 0, 0:8].rearrange("p (g t) -> p g t", g=PASSES),
+                          in_=pdp.rearrange("(g p t) -> p g t", g=PASSES, t=PACK))
+        nc.sync.dma_start(out=powers[:, 1, 0:8], in_=noise.rearrange("(p i) -> p i", i=TILES))
+
+        pilot_raw = {}
+
+        def load_pilots(first, count):
+            raw = keep.tile([P, count, K], BF16, name="pilots%d" % first)
+            nc.sync.dma_start(out=raw[:], in_=pilot_rows[:, first:first + count, :])
+            for i in range(count):
+                pilot_raw[first + i] = raw[:, i, :]
+
+        sub_raw = {}
+
+        def load_sub(g, first, count):
+            raw = keep.tile([P, PACK, count * BANK], BF16, name="sub%d_%d" % (g, first))
+            nc.sync.dma_start(out=raw[:], in_=sub_rows[g][:, :, first * BANK:(first + count) * BANK])
+            for s in range(count):
+                sub_raw[g, first + s] = raw[:, :, s * BANK:(s + 1) * BANK]
+
+        load_pilots(0, 2)
+        scale_rows = to_taps_scales.rearrange("g (q r) n -> r q g n", r=4)
+        for r in range(4):
+            nc.sync.dma_start(out=w_scales[r:P:32, :, :].bitcast(I32), in_=scale_rows[r].bitcast(I32))
+        w_words = keep.tile([P, PASSES, 2 * L], U8, name="w_words", align_bytes=64)
+        nc.sync.dma_start(out=w_words[:].bitcast(I32), in_=to_taps_words.rearrange("g p n -> p g n").bitcast(I32))
+        load_sub(0, 0, 1)
+        load_pilots(2, 2)
+        gain_cols = keep.tile([P, 3, 8], BF16, name="gain_cols")
+        nc.sync.dma_start(out=gain_cols[:], in_=front_end.rearrange("(c p e) -> p c e", p=P, e=8))
+        load_sub(1, 0, 1)
+        load_pilots(4, 2)
+        load_sub(0, 1, 1)
+        load_pilots(6, 2)
+        load_sub(1, 1, 1)
+        load_sub(0, 2, 2)
+        load_sub(1, 2, 2)
+        load_sub(0, 4, 2)
+        load_sub(1, 4, 2)
+
+        parts = keep.tile([P, 3, 16], F32, name="parts")
+        powers_in = powers[:, :, 0:8]
+        nc.vector.tensor_scalar(out=parts[:, 0, :].rearrange("p (a j) -> p a j", a=2), in0=powers_in,
+                                scalar1=1.0 / LN_EDGE, scalar2=LN_EDGE, op0=ALU.max, op1=ALU.min)
+        nc.vector.tensor_scalar(out=parts[:, 1, :].rearrange("p (a j) -> p a j", a=2), in0=powers_in,
+                                scalar1=LN_EDGE, scalar2=1.0 / LN_EDGE, op0=ALU.max, op1=ALU.mult)
+        nc.vector.tensor_scalar(out=parts[:, 2, :].rearrange("p (a j) -> p a j", a=2), in0=powers_in,
+                                scalar1=1.0 / LN_EDGE, scalar2=LN_EDGE, op0=ALU.min, op1=ALU.mult)
+        ln_parts = keep.tile([P, 3, 16], F32, name="ln_parts")
+        nc.scalar.activation(out=ln_parts[:], in_=parts[:], func=ACT.Ln)
+        nc.scalar.activation(out=warm[:, 1:2], in_=one[:], func=ACT.Sigmoid)
+        ln_cols = keep.tile([P, 16], F32, name="ln_cols")
+        nc.vector.tensor_reduce(out=ln_cols[:], in_=ln_parts[:].rearrange("p s j -> p j s"), axis=mybir.AxisListType.X, op=ALU.add)
+        neg_ln_noise = keep.tile([P, TILES], F32, name="neg_ln_noise")
+        nc.vector.tensor_scalar(out=neg_ln_noise[:], in0=ln_cols[:, 8:16], scalar1=-1.0, scalar2=None, op0=ALU.mult)
+
+        def copy_on(engine, dst, src):
+            if engine == "scalar":
+                nc.scalar.copy(out=dst, in_=src)
+            else:
+                nc.vector.tensor_copy(out=dst, in_=src)
+
+        def spread(cols):
+            bank = next_bank()
+            for j in range(4):
+                nc.tensor.transpose(bank[:, j * P:(j + 1) * P], cols[:, j:j + 1].to_broadcast([P, P]), ident[:])
+            return bank
+
+        ln_pdp = keep.tile([P, L], F32, name="ln_pdp")
+        gain = [keep.tile([P, 2 * BANK], BF16, name="gain%d" % c) for c in range(3)]
+
+        def copy_gain(c, bank):
+            nc.scalar.copy(out=gain[c][:].bitcast(F32).rearrange("q (p w) -> q p w", w=4),
+                           in_=bank[:].rearrange("q (w p) -> q p w", w=4))
+
+        def turn(words, stepped):
+            bank = next_bank()
+            for g in range(PASSES):
+                for u in range(2):
+                    if stepped:
+                        src = words[:, 256 * g + u:256 * (g + 1):2]
+                    else:
+                        src = words[:, 256 * g + P * u:256 * g + P * (u + 1)]
+                    nc.tensor.transpose(bank[:, (2 * g + u) * P:(2 * g + u + 1) * P], src, ident[:])
+            return bank
+
+        def gather_words(engine, bank, tag):
+            grouped = work.tile([P, PASSES * P * PACK], BF16, name=tag, tag=tag, bufs=3, align_bytes=64)
+            copy_on(engine, grouped[:].bitcast(F32).rearrange("p (g m u) -> p g m u", g=PASSES, u=2),
+                    bank[:].rearrange("p (g u m) -> p g m u", g=PASSES, u=2))
+            return grouped
+
+        pilot_mx, clean_mx, sub_mx = {}, {}, {}
+        shrink, clean, sub_grouped = {}, {}, {}
+
+        def quantize(grouped, pool, name, tag, fmt):
+            width = grouped.shape[1] // PACK
+            codes = pool.tile([P, width], U32, name=name + "_codes", tag=tag + "_codes", align_bytes=64)
+            scales = pool.tile([P, width], U8, name=name + "_scales", tag=tag + "_scales", align_bytes=64)
+            nc.vector.quantize_mx(out=codes[:].bitcast(fmt), scales=scales[:], in_=grouped[:])
+            return codes, scales
+
+        def make_shrink(i):
+            shrink[i] = work.tile([P, L], F32, name="shrink", tag="shrink", bufs=2)
+            nc.scalar.activation(out=shrink[i][:], in_=ln_pdp[:], func=ACT.Sigmoid, bias=neg_ln_noise[:, i:i + 1])
+
+        def taps_matmul(i, h):
+            bank = next_bank()
+            codes, scales = pilot_mx[i]
+            for g in range(PASSES):
+                nc.tensor.matmul_mx(out=bank[:], lhsT=codes[:, g * P:(g + 1) * P].bitcast(E4M3), lhsT_scale=scales[:, g * P:(g + 1) * P],
+                                    rhs=w_words[:, g, 2 * h * BANK:2 * (h + 1) * BANK].bitcast(E2M1),
+                                    rhs_scale=w_scales[:, g, h * BANK:(h + 1) * BANK], start=(g == 0), stop=(g == PASSES - 1))
+            return bank
+
+        def shrink_taps(i, h, bank):
+            cols = slice(h * BANK, (h + 1) * BANK)
+            nc.vector.tensor_tensor(out=clean[i][:, cols].rearrange("m (u p e) -> m u p e", u=2, e=2),
+                                    in0=bank[:].rearrange("m (p u e) -> m u p e", u=2, e=2),
+                                    in1=shrink[i][:, cols].rearrange("m (u p e) -> m u p e", u=2, e=2), op=ALU.mult)
+
+        half = BANK // 2
+
+        def interleave(engine, g, s, first, count):
+            if (g, s) not in sub_grouped:
+                sub_grouped[g, s] = work.tile([P, BANK * PACK], BF16, name="sub_grouped", tag="sub_grouped", bufs=3, align_bytes=64)
+            dst = sub_grouped[g, s][:, first * PACK:(first + count) * PACK]
+            copy_on(engine, dst.rearrange("p (c i t) -> p c t i", i=4, t=PACK),
+                    sub_raw[g, s][:, :, first:first + count].rearrange("p t (c i) -> p c t i", i=4))
+
+        def quantize_sub(g, s):
+            name = "sub_mx%d_%d" % (g, s)
+            sub_mx[g, s] = quantize(sub_grouped[g, s], keep, name, name, E4M3)
+
+        def interleave_half(g, s, h):
+            grouped = work.tile([P, half * PACK], BF16, name="half_grouped", tag="half_grouped", bufs=1, align_bytes=64)
+            nc.gpsimd.tensor_scalar(out=grouped[:].rearrange("p (c t) -> p c t", t=PACK),
+                                    in0=sub_raw[g, s][:, :, h * half:(h + 1) * half].rearrange("p t c -> p c t"),
+                                    scalar1=1.0, scalar2=0.0, op0=ALU.mult, op1=ALU.add)
+            return g, s, h, grouped
+
+        def quantize_half(g, s, h, grouped):
+            if (g, s) not in sub_mx:
+                name = "sub_mx%d_%d" % (g, s)
+                sub_mx[g, s] = (keep.tile([P, BANK], U32, name=name + "_codes", align_bytes=64),
+                                keep.tile([P, BANK], U8, name=name + "_scales", align_bytes=64))
+            codes, scales = sub_mx[g, s]
+            cols = slice(h * half, (h + 1) * half)
+            nc.vector.quantize_mx(out=codes[:, cols].bitcast(E4M3), scales=scales[:, cols], in_=grouped[:])
+
+        def out_matmul(i, s):
+            bank = next_bank()
+            codes, scales = clean_mx[i]
+            for g in range(PASSES):
+                nc.tensor.matmul_mx(out=bank[:], lhsT=codes[:, g * P:(g + 1) * P].bitcast(E5M2), lhsT_scale=scales[:, g * P:(g + 1) * P],
+                                    rhs=sub_mx[g, s][0][:].bitcast(E4M3), rhs_scale=sub_mx[g, s][1][:],
+                                    start=(g == 0), stop=(g == PASSES - 1))
+            return bank
+
+        def out_job(i, first, count, shared=()):
+            banks = [out_matmul(i, first + j) for j in range(count)]
+            result = work.tile([P, 2 * BANK], F32, name="result", tag="result", bufs=6)
+            for j, bank in enumerate(banks):
+                s = first + j
+                dst = result[:, j * BANK:(j + 1) * BANK]
+                factor = gain[s // 2][:, (s % 2) * BANK:(s % 2 + 1) * BANK]
+                if j in shared:
+                    nc.scalar.copy(out=dst, in_=bank[:])
+                    nc.gpsimd.tensor_tensor(out=dst, in0=dst, in1=factor, op=ALU.mult)
+                else:
+                    nc.vector.tensor_tensor(out=dst, in0=bank[:], in1=factor, op=ALU.mult)
+            nc.sync.dma_start(out=out_rows[:, i, first * BANK:(first + count) * BANK], in_=result[:, 0:count * BANK])
+
+        first_bank = turn(pilot_raw[0].bitcast(F32), True)
+        ln_banks = [spread(ln_cols[:, 4 * g:4 * g + 4]) for g in range(PASSES)]
+        pilot_bank = turn(pilot_raw[1].bitcast(F32), True)
+        pilot_mx[0] = quantize(gather_words("vector", first_bank, "pilot_grouped"), work, "pilot", "pilot", E4M3)
+        for g, engine in enumerate(("vector", "scalar")):
+            copy_on(engine, ln_pdp[:, g * BANK:(g + 1) * BANK].rearrange("q (u p e) -> q u p e", u=2, e=2),
+                    ln_banks[g][:].rearrange("q (u e p) -> q u p e", u=2, e=2))
+        make_shrink(0)
+        interleave("vector", 0, 0, 0, BANK)
+
+        quarter = BANK // 4
+        gain_steps = (1, 7, 8)
+        halves = [(g, s, h) for g, s in ((1, 0), (1, 1), (0, 2), (1, 2)) for h in range(2)]
+        pending = interleave_half(*halves[0])
+        pilot_banks = {1: pilot_bank}
+        pilot_grouped = {}
+
+        def quantize_pilots(i):
+            pilot_mx[i] = quantize(pilot_grouped[i], work, "pilot", "pilot", E4M3)
+
+        def quantize_clean(i, grouped):
+            name = "clean_mx%d" % i
+            clean_mx[i] = quantize(grouped, keep, name, name, E5M2)
+
+        for step in range(TILES + 2):
+            ahead, behind = step + 1, step - 2
+            for i in sorted(pilot_banks):
+                pilot_grouped[i] = gather_words("scalar", pilot_banks[i], "pilot_grouped")
+            pilot_banks = {}
+            if behind >= 0:
+                clean_grouped = gather_words("scalar", clean_bank, "clean_grouped")
+            if step - 1 in gain_steps:
+                copy_gain(gain_steps.index(step - 1), gain_bank)
+            if 3 <= step <= 6:
+                interleave("scalar", 0, 1, (step - 3) * quarter, quarter)
+            if ahead < TILES:
+                make_shrink(ahead)
+            if step < TILES:
+                taps = [taps_matmul(step, h) for h in range(2)]
+                clean[step] = work.tile([P, L], BF16, name="clean", tag="clean")
+                shrink_taps(step, 0, taps[0])
+                if step < 2:
+                    quantize_pilots(step + 1)
+                shrink_taps(step, 1, taps[1])
+            if 3 <= step < TILES:
+                out_job(step - 3, 0, 1)
+            if 2 < step + 2 < TILES:
+                quantize_pilots(step + 2)
+            if 0 <= behind < TILES - 2:
+                quantize_clean(behind, clean_grouped)
+            if step == 0:
+                quantize_sub(0, 0)
+            if step == 6:
+                quantize_sub(0, 1)
+            if 1 <= step < len(halves):
+                quantize_half(*pending)
+                pending = interleave_half(*halves[step])
+            for i in range(2 if step == 0 else step + 3, min(step + 4, TILES)):
+                pilot_banks[i] = turn(pilot_raw[i].bitcast(F32), True)
+            if 1 <= step <= TILES:
+                clean_bank = turn(clean[step - 1][:].bitcast(F32), False)
+            if step in gain_steps:
+                gain_bank = spread(gain_cols[:, gain_steps.index(step), :].bitcast(F32))
+            if step == 7:
+                interleave("scalar", 0, 3, 0, BANK)
+            if step == 8:
+                interleave("scalar", 1, 3, 0, BANK)
+                out_job(0, 1, 1)
+                out_job(1, 1, 1)
+                out_job(2, 1, 1)
+                quantize_clean(behind, clean_grouped)
+                quantize_sub(0, 3)
+                quantize_half(*pending)
+                pending = interleave_half(0, 4, 0)
+                out_job(5, 0, 2)
+            if step == 9:
+                out_job(3, 1, 1)
+                out_job(4, 1, 1)
+                quantize_clean(behind, clean_grouped)
+                quantize_sub(1, 3)
+                quantize_half(*pending)
+                pending = interleave_half(0, 4, 1)
+                out_job(6, 0, 2)
+
+        late = [(1, 4), (0, 5), (1, 5)]
+        interleave("scalar", 1, 4, 0, half)
+        out_job(7, 0, 2)
+        quantize_half(*pending)
+        for i in range(TILES):
+            if i < 5:
+                interleave("scalar", *late[(i + 1) // 2], ((i + 1) % 2) * half, half)
+            out_job(i, 2, 2, (0,) if i in SHARED_A else ())
+            if i in (0, 2, 4):
+                quantize_sub(*late[i // 2])
+        for i in range(TILES - 1):
+            out_job(i, 4, 2, (0,) if i in SHARED_B else ())
+        out_job(TILES - 1, 4, 1)
+        out_job(TILES - 1, 5, 1)

@@ -24,8 +24,8 @@ TILES = M // P
 BANK = 512
 STRIPS = N // BANK
 LN_EDGE = 2.0 ** 64
-SHARED_A = (1, 3, 5, 6)
-SHARED_B = (0, 1, 2, 4, 5)
+SH = [(0,), (0,), (), (0,), ()]
+SHARED_B = ()
 
 
 def tile_delay_domain_denoising_s9_kernel(tc, pilots, to_taps_words, to_taps_scales, pdp, noise, to_sub, front_end, out):
@@ -85,13 +85,13 @@ def tile_delay_domain_denoising_s9_kernel(tc, pilots, to_taps_words, to_taps_sca
         nc.sync.dma_start(out=w_words[:].bitcast(I32), in_=to_taps_words.rearrange("g p n -> p g n").bitcast(I32))
         load_sub(0, 0, 1)
         load_pilots(2, 2)
-        gain_cols = keep.tile([P, 3, 8], BF16, name="gain_cols")
-        nc.sync.dma_start(out=gain_cols[:], in_=front_end.rearrange("(c p e) -> p c e", p=P, e=8))
         load_sub(1, 0, 1)
         load_pilots(4, 2)
+        gain_cols = keep.tile([P, 3, 8], BF16, name="gain_cols")
+        nc.sync.dma_start(out=gain_cols[:], in_=front_end.rearrange("(c p e) -> p c e", p=P, e=8))
         load_sub(0, 1, 1)
-        load_pilots(6, 2)
         load_sub(1, 1, 1)
+        load_pilots(6, 2)
         load_sub(0, 2, 2)
         load_sub(1, 2, 2)
         load_sub(0, 4, 2)
@@ -159,9 +159,10 @@ def tile_delay_domain_denoising_s9_kernel(tc, pilots, to_taps_words, to_taps_sca
             nc.vector.quantize_mx(out=codes[:].bitcast(fmt), scales=scales[:], in_=grouped[:])
             return codes, scales
 
-        def make_shrink(i):
-            shrink[i] = work.tile([P, L], F32, name="shrink", tag="shrink", bufs=2)
-            nc.scalar.activation(out=shrink[i][:], in_=ln_pdp[:], func=ACT.Sigmoid, bias=neg_ln_noise[:, i:i + 1])
+        def make_shrink(i, cols):
+            if i not in shrink:
+                shrink[i] = work.tile([P, L], F32, name="shrink", tag="shrink", bufs=2)
+            nc.scalar.activation(out=shrink[i][:, cols], in_=ln_pdp[:, cols], func=ACT.Sigmoid, bias=neg_ln_noise[:, i:i + 1])
 
         def taps_matmul(i, h):
             bank = next_bank()
@@ -182,7 +183,7 @@ def tile_delay_domain_denoising_s9_kernel(tc, pilots, to_taps_words, to_taps_sca
 
         def interleave(engine, g, s, first, count):
             if (g, s) not in sub_grouped:
-                sub_grouped[g, s] = work.tile([P, BANK * PACK], BF16, name="sub_grouped", tag="sub_grouped", bufs=3, align_bytes=64)
+                sub_grouped[g, s] = work.tile([P, BANK * PACK], BF16, name="sub_grouped", tag="sub_grouped", bufs=4, align_bytes=64)
             dst = sub_grouped[g, s][:, first * PACK:(first + count) * PACK]
             copy_on(engine, dst.rearrange("p (c i t) -> p c t i", i=4, t=PACK),
                     sub_raw[g, s][:, :, first:first + count].rearrange("p t (c i) -> p c t i", i=4))
@@ -218,7 +219,7 @@ def tile_delay_domain_denoising_s9_kernel(tc, pilots, to_taps_words, to_taps_sca
 
         def out_job(i, first, count, shared=()):
             banks = [out_matmul(i, first + j) for j in range(count)]
-            result = work.tile([P, 2 * BANK], F32, name="result", tag="result", bufs=6)
+            result = work.tile([P, 2 * BANK], F32, name="result", tag="result", bufs=9)
             for j, bank in enumerate(banks):
                 s = first + j
                 dst = result[:, j * BANK:(j + 1) * BANK]
@@ -233,17 +234,18 @@ def tile_delay_domain_denoising_s9_kernel(tc, pilots, to_taps_words, to_taps_sca
         first_bank = turn(pilot_raw[0].bitcast(F32), True)
         ln_banks = [spread(ln_cols[:, 4 * g:4 * g + 4]) for g in range(PASSES)]
         pilot_bank = turn(pilot_raw[1].bitcast(F32), True)
-        pilot_mx[0] = quantize(gather_words("vector", first_bank, "pilot_grouped"), work, "pilot", "pilot", E4M3)
+        first_grouped = gather_words("vector", first_bank, "pilot_grouped")
+        pilot_mx[0] = quantize(first_grouped, work, "pilot", "pilot", E4M3)
         for g, engine in enumerate(("vector", "scalar")):
             copy_on(engine, ln_pdp[:, g * BANK:(g + 1) * BANK].rearrange("q (u p e) -> q u p e", u=2, e=2),
                     ln_banks[g][:].rearrange("q (u e p) -> q u p e", u=2, e=2))
-        make_shrink(0)
+        for g in range(PASSES):
+            make_shrink(0, slice(g * BANK, (g + 1) * BANK))
         interleave("vector", 0, 0, 0, BANK)
 
         quarter = BANK // 4
-        gain_steps = (1, 7, 8)
-        halves = [(g, s, h) for g, s in ((1, 0), (1, 1), (0, 2), (1, 2)) for h in range(2)]
-        pending = interleave_half(*halves[0])
+        gain_steps = (2,)
+        halves = [(g, s, h) for g, s in ((1, 0), (0, 1), (0, 2), (1, 2), (0, 4)) for h in range(2)]
         pilot_banks = {1: pilot_bank}
         pilot_grouped = {}
 
@@ -254,7 +256,7 @@ def tile_delay_domain_denoising_s9_kernel(tc, pilots, to_taps_words, to_taps_sca
             name = "clean_mx%d" % i
             clean_mx[i] = quantize(grouped, keep, name, name, E5M2)
 
-        for step in range(TILES + 2):
+        for step in range(TILES):
             ahead, behind = step + 1, step - 2
             for i in sorted(pilot_banks):
                 pilot_grouped[i] = gather_words("scalar", pilot_banks[i], "pilot_grouped")
@@ -263,10 +265,16 @@ def tile_delay_domain_denoising_s9_kernel(tc, pilots, to_taps_words, to_taps_sca
                 clean_grouped = gather_words("scalar", clean_bank, "clean_grouped")
             if step - 1 in gain_steps:
                 copy_gain(gain_steps.index(step - 1), gain_bank)
-            if 3 <= step <= 6:
-                interleave("scalar", 0, 1, (step - 3) * quarter, quarter)
+            if step in (3, 4):
+                interleave("scalar", 1, 1, (step - 2) * quarter, (step - 2) * quarter)
             if ahead < TILES:
-                make_shrink(ahead)
+                make_shrink(ahead, slice(0, L))
+            if step == 2:
+                interleave("scalar", 1, 1, 0, quarter)
+            if step in (5, 6):
+                interleave("scalar", 0, 3, (step - 5) * half, half)
+            if step == 6:
+                interleave("scalar", 1, 3, 0, half)
             if step < TILES:
                 taps = [taps_matmul(step, h) for h in range(2)]
                 clean[step] = work.tile([P, L], BF16, name="clean", tag="clean")
@@ -275,17 +283,20 @@ def tile_delay_domain_denoising_s9_kernel(tc, pilots, to_taps_words, to_taps_sca
                     quantize_pilots(step + 1)
                 shrink_taps(step, 1, taps[1])
             if 3 <= step < TILES:
-                out_job(step - 3, 0, 1)
+                out_job(step - 3, 0, 1 if step < 5 else 2)
             if 2 < step + 2 < TILES:
                 quantize_pilots(step + 2)
-            if 0 <= behind < TILES - 2:
+            if behind >= 0:
                 quantize_clean(behind, clean_grouped)
-            if step == 0:
+            if step == 1:
                 quantize_sub(0, 0)
-            if step == 6:
-                quantize_sub(0, 1)
-            if 1 <= step < len(halves):
+            if step == 4:
+                quantize_sub(1, 1)
+            if step == 7:
+                quantize_sub(0, 3)
+            if 1 <= step < TILES - 1:
                 quantize_half(*pending)
+            if step < TILES - 1:
                 pending = interleave_half(*halves[step])
             for i in range(2 if step == 0 else step + 3, min(step + 4, TILES)):
                 pilot_banks[i] = turn(pilot_raw[i].bitcast(F32), True)
@@ -293,37 +304,42 @@ def tile_delay_domain_denoising_s9_kernel(tc, pilots, to_taps_words, to_taps_sca
                 clean_bank = turn(clean[step - 1][:].bitcast(F32), False)
             if step in gain_steps:
                 gain_bank = spread(gain_cols[:, gain_steps.index(step), :].bitcast(F32))
-            if step == 7:
-                interleave("scalar", 0, 3, 0, BANK)
-            if step == 8:
-                interleave("scalar", 1, 3, 0, BANK)
-                out_job(0, 1, 1)
-                out_job(1, 1, 1)
-                out_job(2, 1, 1)
-                quantize_clean(behind, clean_grouped)
-                quantize_sub(0, 3)
-                quantize_half(*pending)
-                pending = interleave_half(0, 4, 0)
-                out_job(5, 0, 2)
-            if step == 9:
-                out_job(3, 1, 1)
-                out_job(4, 1, 1)
-                quantize_clean(behind, clean_grouped)
-                quantize_sub(1, 3)
-                quantize_half(*pending)
-                pending = interleave_half(0, 4, 1)
-                out_job(6, 0, 2)
 
-        late = [(1, 4), (0, 5), (1, 5)]
-        interleave("scalar", 1, 4, 0, half)
-        out_job(7, 0, 2)
+        last_bank = turn(clean[TILES - 1][:].bitcast(F32), False)
+        gain_bank = spread(gain_cols[:, 1, :].bitcast(F32))
+        last_grouped = [gather_words("scalar", bank, "clean_grouped") for bank in (clean_bank, last_bank)]
+        quantize_clean(TILES - 2, last_grouped[0])
+        quantize_clean(TILES - 1, last_grouped[1])
         quantize_half(*pending)
-        for i in range(TILES):
-            if i < 5:
-                interleave("scalar", *late[(i + 1) // 2], ((i + 1) % 2) * half, half)
-            out_job(i, 2, 2, (0,) if i in SHARED_A else ())
-            if i in (0, 2, 4):
-                quantize_sub(*late[i // 2])
+        pending = interleave_half(*halves[7])
+        interleave("scalar", 1, 3, half, half)
+        copy_gain(1, gain_bank)
+        interleave("scalar", 1, 4, 0, BANK)
+        out_job(0, 1, 1)
+        out_job(1, 1, 1)
+        out_job(5, 0, 2)
+        quantize_sub(1, 3)
+        quantize_half(*pending)
+        pending = interleave_half(*halves[8])
+        out_job(6, 0, 2)
+        out_job(7, 0, 2)
+        out_job(0, 2, 2, SH[0])
+        interleave("scalar", 0, 5, 0, BANK)
+        quantize_sub(1, 4)
+        quantize_half(*pending)
+        pending = interleave_half(*halves[9])
+        out_job(1, 2, 2)
+        out_job(2, 2, 2)
+        out_job(3, 2, 2, SH[1])
+        interleave("scalar", 1, 5, 0, BANK)
+        quantize_sub(0, 5)
+        quantize_half(*pending)
+        copy_gain(2, spread(gain_cols[:, 2, :].bitcast(F32)))
+        out_job(4, 2, 2, SH[2])
+        out_job(5, 2, 2)
+        quantize_sub(1, 5)
+        out_job(6, 2, 2, SH[3])
+        out_job(7, 2, 2, SH[4])
         for i in range(TILES - 1):
             out_job(i, 4, 2, (0,) if i in SHARED_B else ())
         out_job(TILES - 1, 4, 1)

@@ -24,8 +24,8 @@ TILES = M // P
 BANK = 512
 STRIPS = N // BANK
 LN_EDGE = 2.0 ** 64
-SH = [(0,), (0,), (), (0,), ()]
-SHARED_B = ()
+QN = 7
+LAST = 15
 
 
 def tile_delay_domain_denoising_s9_kernel(tc, pilots, to_taps_words, to_taps_scales, pdp, noise, to_sub, front_end, out):
@@ -77,12 +77,13 @@ def tile_delay_domain_denoising_s9_kernel(tc, pilots, to_taps_words, to_taps_sca
             for s in range(count):
                 sub_raw[g, first + s] = raw[:, :, s * BANK:(s + 1) * BANK]
 
-        load_pilots(0, 2)
+        load_pilots(0, 1)
         scale_rows = to_taps_scales.rearrange("g (q r) n -> r q g n", r=4)
         for r in range(4):
             nc.sync.dma_start(out=w_scales[r:P:32, :, :].bitcast(I32), in_=scale_rows[r].bitcast(I32))
         w_words = keep.tile([P, PASSES, 2 * L], U8, name="w_words", align_bytes=64)
         nc.sync.dma_start(out=w_words[:].bitcast(I32), in_=to_taps_words.rearrange("g p n -> p g n").bitcast(I32))
+        load_pilots(1, 1)
         load_sub(0, 0, 1)
         load_pilots(2, 2)
         load_sub(1, 0, 1)
@@ -128,9 +129,9 @@ def tile_delay_domain_denoising_s9_kernel(tc, pilots, to_taps_words, to_taps_sca
         ln_pdp = keep.tile([P, L], F32, name="ln_pdp")
         gain = [keep.tile([P, 2 * BANK], BF16, name="gain%d" % c) for c in range(3)]
 
-        def copy_gain(c, bank):
-            nc.scalar.copy(out=gain[c][:].bitcast(F32).rearrange("q (p w) -> q p w", w=4),
-                           in_=bank[:].rearrange("q (w p) -> q p w", w=4))
+        def copy_gain(engine, c, bank):
+            copy_on(engine, gain[c][:].bitcast(F32).rearrange("q (p w) -> q p w", w=4),
+                    bank[:].rearrange("q (w p) -> q p w", w=4))
 
         def turn(words, stepped):
             bank = next_bank()
@@ -244,7 +245,7 @@ def tile_delay_domain_denoising_s9_kernel(tc, pilots, to_taps_words, to_taps_sca
         interleave("vector", 0, 0, 0, BANK)
 
         quarter = BANK // 4
-        gain_steps = (2,)
+        gain_steps = (1,)
         halves = [(g, s, h) for g, s in ((1, 0), (0, 1), (0, 2), (1, 2), (0, 4)) for h in range(2)]
         pilot_banks = {1: pilot_bank}
         pilot_grouped = {}
@@ -263,8 +264,6 @@ def tile_delay_domain_denoising_s9_kernel(tc, pilots, to_taps_words, to_taps_sca
             pilot_banks = {}
             if behind >= 0:
                 clean_grouped = gather_words("scalar", clean_bank, "clean_grouped")
-            if step - 1 in gain_steps:
-                copy_gain(gain_steps.index(step - 1), gain_bank)
             if step in (3, 4):
                 interleave("scalar", 1, 1, (step - 2) * quarter, (step - 2) * quarter)
             if ahead < TILES:
@@ -281,15 +280,17 @@ def tile_delay_domain_denoising_s9_kernel(tc, pilots, to_taps_words, to_taps_sca
                 shrink_taps(step, 0, taps[0])
                 if step < 2:
                     quantize_pilots(step + 1)
+                if step == 0:
+                    quantize_sub(0, 0)
                 shrink_taps(step, 1, taps[1])
+            if step == 2:
+                copy_gain("vector", 0, gain_bank)
             if 3 <= step < TILES:
-                out_job(step - 3, 0, 1 if step < 5 else 2)
+                out_job(step - 3, 0, 1 if step < 6 else 2)
             if 2 < step + 2 < TILES:
                 quantize_pilots(step + 2)
             if behind >= 0:
                 quantize_clean(behind, clean_grouped)
-            if step == 1:
-                quantize_sub(0, 0)
             if step == 4:
                 quantize_sub(1, 1)
             if step == 7:
@@ -313,34 +314,27 @@ def tile_delay_domain_denoising_s9_kernel(tc, pilots, to_taps_words, to_taps_sca
         quantize_half(*pending)
         pending = interleave_half(*halves[7])
         interleave("scalar", 1, 3, half, half)
-        copy_gain(1, gain_bank)
+        copy_gain("scalar", 1, gain_bank)
         interleave("scalar", 1, 4, 0, BANK)
-        out_job(0, 1, 1)
-        out_job(1, 1, 1)
-        out_job(5, 0, 2)
+        for i in range(3):
+            out_job(i, 1, 1)
         quantize_sub(1, 3)
         quantize_half(*pending)
         pending = interleave_half(*halves[8])
-        out_job(6, 0, 2)
-        out_job(7, 0, 2)
-        out_job(0, 2, 2, SH[0])
-        interleave("scalar", 0, 5, 0, BANK)
-        quantize_sub(1, 4)
-        quantize_half(*pending)
-        pending = interleave_half(*halves[9])
-        out_job(1, 2, 2)
-        out_job(2, 2, 2)
-        out_job(3, 2, 2, SH[1])
-        interleave("scalar", 1, 5, 0, BANK)
-        quantize_sub(0, 5)
-        quantize_half(*pending)
-        copy_gain(2, spread(gain_cols[:, 2, :].bitcast(F32)))
-        out_job(4, 2, 2, SH[2])
-        out_job(5, 2, 2)
-        quantize_sub(1, 5)
-        out_job(6, 2, 2, SH[3])
-        out_job(7, 2, 2, SH[4])
-        for i in range(TILES - 1):
-            out_job(i, 4, 2, (0,) if i in SHARED_B else ())
+        pairs = [(i, 0) for i in range(5, TILES)] + [(i, first) for first in (2, 4) for i in range(TILES)]
+        for n, (i, first) in enumerate(pairs[:-1]):
+            out_job(i, first, 2, (0,) if n % 3 == 2 and n < LAST else ())
+            if n in (2, 5):
+                interleave("scalar", n // 3, 5, 0, BANK)
+            if n == 2:
+                quantize_sub(1, 4)
+                quantize_half(*pending)
+                pending = interleave_half(*halves[9])
+            if n == 5:
+                quantize_sub(0, 5)
+                quantize_half(*pending)
+            if n == QN:
+                quantize_sub(1, 5)
+                copy_gain("scalar", 2, spread(gain_cols[:, 2, :].bitcast(F32)))
         out_job(TILES - 1, 4, 1)
         out_job(TILES - 1, 5, 1)

@@ -22,13 +22,20 @@ PACK = 4
 PASSES = 2
 TILES = M // P
 BANK = 512
-STRIPS = N // BANK
+BANKS = 8
+HALF = BANK // 2
+QUARTER = BANK // 4
 LN_EDGE = 2.0 ** 64
-QN = 7
-LAST = 15
+
+OUT_LAG = 3
+FIRST_WIDE_STEP = 6
+SHARE_EVERY = 3
+SHARE_UNTIL = 15
+LAST_UNIT_AFTER = 7
 
 
-def tile_delay_domain_denoising_s9_kernel(tc, pilots, to_taps_words, to_taps_scales, pdp, noise, to_sub, front_end, out):
+def tile_delay_domain_denoising_s9_kernel(tc, pilots, to_taps_words, to_taps_scales, pdp, noise, to_sub,
+                                                     front_end, out):
     nc = tc.nc
     pilot_rows = pilots.rearrange("(p i) k -> p i k", i=TILES)
     out_rows = out.rearrange("(p i) n -> p i n", i=TILES)
@@ -43,16 +50,12 @@ def tile_delay_domain_denoising_s9_kernel(tc, pilots, to_taps_words, to_taps_sca
         banks_taken = []
 
         def next_bank():
-            tag = "bank%d" % (len(banks_taken) % 8)
+            tag = "bank%d" % (len(banks_taken) % BANKS)
             banks_taken.append(tag)
             return psum.tile([P, BANK], F32, name=tag, tag=tag)
 
         w_scales = keep.tile([P, PASSES, L], U8, name="w_scales", align_bytes=64)
         nc.vector.memset(w_scales[:].rearrange("p g n -> p (g n)").bitcast(I32), 0)
-        one = keep.tile([P, 1], F32, name="one")
-        nc.vector.memset(one[:], 1.0)
-        warm = keep.tile([P, 2], F32, name="warm")
-        nc.scalar.activation(out=warm[:, 0:1], in_=one[:], func=ACT.Ln)
         ident = keep.tile([P, P], F32, name="ident")
         make_identity(nc, ident[:])
 
@@ -93,32 +96,25 @@ def tile_delay_domain_denoising_s9_kernel(tc, pilots, to_taps_words, to_taps_sca
         load_sub(0, 1, 1)
         load_sub(1, 1, 1)
         load_pilots(6, 2)
-        load_sub(0, 2, 2)
-        load_sub(1, 2, 2)
-        load_sub(0, 4, 2)
-        load_sub(1, 4, 2)
+        for first in (2, 4):
+            for g in range(PASSES):
+                load_sub(g, first, 2)
 
-        parts = keep.tile([P, 3, 16], F32, name="parts")
-        powers_in = powers[:, :, 0:8]
-        nc.vector.tensor_scalar(out=parts[:, 0, :].rearrange("p (a j) -> p a j", a=2), in0=powers_in,
-                                scalar1=1.0 / LN_EDGE, scalar2=LN_EDGE, op0=ALU.max, op1=ALU.min)
-        nc.vector.tensor_scalar(out=parts[:, 1, :].rearrange("p (a j) -> p a j", a=2), in0=powers_in,
-                                scalar1=LN_EDGE, scalar2=1.0 / LN_EDGE, op0=ALU.max, op1=ALU.mult)
-        nc.vector.tensor_scalar(out=parts[:, 2, :].rearrange("p (a j) -> p a j", a=2), in0=powers_in,
-                                scalar1=1.0 / LN_EDGE, scalar2=LN_EDGE, op0=ALU.min, op1=ALU.mult)
-        ln_parts = keep.tile([P, 3, 16], F32, name="ln_parts")
-        nc.scalar.activation(out=ln_parts[:], in_=parts[:], func=ACT.Ln)
-        nc.scalar.activation(out=warm[:, 1:2], in_=one[:], func=ACT.Sigmoid)
+        factors = keep.tile([P, 3, 16], F32, name="factors")
+        splits = ((1.0 / LN_EDGE, LN_EDGE, ALU.max, ALU.min), (LN_EDGE, 1.0 / LN_EDGE, ALU.max, ALU.mult),
+                  (1.0 / LN_EDGE, LN_EDGE, ALU.min, ALU.mult))
+        for f, (first_scalar, second_scalar, first_op, second_op) in enumerate(splits):
+            nc.vector.tensor_scalar(out=factors[:, f, :].rearrange("p (a j) -> p a j", a=2), in0=powers[:, :, 0:8],
+                                    scalar1=first_scalar, scalar2=second_scalar, op0=first_op, op1=second_op)
+        ln_factors = keep.tile([P, 3, 16], F32, name="ln_factors")
+        nc.scalar.activation(out=ln_factors[:], in_=factors[:], func=ACT.Ln)
         ln_cols = keep.tile([P, 16], F32, name="ln_cols")
-        nc.vector.tensor_reduce(out=ln_cols[:], in_=ln_parts[:].rearrange("p s j -> p j s"), axis=mybir.AxisListType.X, op=ALU.add)
+        nc.vector.tensor_reduce(out=ln_cols[:], in_=ln_factors[:].rearrange("p f j -> p j f"),
+                                axis=mybir.AxisListType.X, op=ALU.add)
         neg_ln_noise = keep.tile([P, TILES], F32, name="neg_ln_noise")
         nc.vector.tensor_scalar(out=neg_ln_noise[:], in0=ln_cols[:, 8:16], scalar1=-1.0, scalar2=None, op0=ALU.mult)
 
-        def copy_on(engine, dst, src):
-            if engine == "scalar":
-                nc.scalar.copy(out=dst, in_=src)
-            else:
-                nc.vector.tensor_copy(out=dst, in_=src)
+        on_scalar, on_vector = nc.scalar.copy, nc.vector.tensor_copy
 
         def spread(cols):
             bank = next_bank()
@@ -129,49 +125,64 @@ def tile_delay_domain_denoising_s9_kernel(tc, pilots, to_taps_words, to_taps_sca
         ln_pdp = keep.tile([P, L], F32, name="ln_pdp")
         gain = [keep.tile([P, 2 * BANK], BF16, name="gain%d" % c) for c in range(3)]
 
-        def copy_gain(engine, c, bank):
-            copy_on(engine, gain[c][:].bitcast(F32).rearrange("q (p w) -> q p w", w=4),
-                    bank[:].rearrange("q (w p) -> q p w", w=4))
+        def spread_gain(c):
+            return spread(gain_cols[:, c, :].bitcast(F32))
 
-        def turn(words, stepped):
+        def copy_gain(copy, c, bank):
+            copy(out=gain[c][:].bitcast(F32).rearrange("q (p j) -> q p j", j=4),
+                 in_=bank[:].rearrange("q (j p) -> q p j", j=4))
+
+        def turn(pair_columns):
             bank = next_bank()
             for g in range(PASSES):
                 for u in range(2):
-                    if stepped:
-                        src = words[:, 256 * g + u:256 * (g + 1):2]
-                    else:
-                        src = words[:, 256 * g + P * u:256 * g + P * (u + 1)]
-                    nc.tensor.transpose(bank[:, (2 * g + u) * P:(2 * g + u + 1) * P], src, ident[:])
+                    nc.tensor.transpose(bank[:, (2 * g + u) * P:(2 * g + u + 1) * P], pair_columns(g, u), ident[:])
             return bank
 
-        def gather_words(engine, bank, tag):
-            grouped = work.tile([P, PASSES * P * PACK], BF16, name=tag, tag=tag, bufs=3, align_bytes=64)
-            copy_on(engine, grouped[:].bitcast(F32).rearrange("p (g m u) -> p g m u", g=PASSES, u=2),
-                    bank[:].rearrange("p (g u m) -> p g m u", g=PASSES, u=2))
+        def turn_pilots(i):
+            pairs = pilot_raw[i].bitcast(F32)
+            return turn(lambda g, u: pairs[:, HALF * g + u:HALF * (g + 1):2])
+
+        def turn_clean(i):
+            pairs = clean[i][:].bitcast(F32)
+            return turn(lambda g, u: pairs[:, HALF * g + P * u:HALF * g + P * (u + 1)])
+
+        def group_pairs(copy, bank, tag):
+            grouped = work.tile([P, PASSES * P * PACK], BF16, name=tag, tag=tag, align_bytes=64)
+            copy(out=grouped[:].bitcast(F32).rearrange("p (g m u) -> p g m u", g=PASSES, u=2),
+                 in_=bank[:].rearrange("p (g u m) -> p g m u", g=PASSES, u=2))
             return grouped
 
-        pilot_mx, clean_mx, sub_mx = {}, {}, {}
-        shrink, clean, sub_grouped = {}, {}, {}
+        pilot_grouped, pilot_mx, shrink, clean, clean_mx, sub_grouped, sub_mx = {}, {}, {}, {}, {}, {}, {}
 
-        def quantize(grouped, pool, name, tag, fmt):
+        def quantize(grouped, pool, name, fmt):
             width = grouped.shape[1] // PACK
-            codes = pool.tile([P, width], U32, name=name + "_codes", tag=tag + "_codes", align_bytes=64)
-            scales = pool.tile([P, width], U8, name=name + "_scales", tag=tag + "_scales", align_bytes=64)
+            codes = pool.tile([P, width], U32, name=name + "_codes", tag=name + "_codes", align_bytes=64)
+            scales = pool.tile([P, width], U8, name=name + "_scales", tag=name + "_scales", align_bytes=64)
             nc.vector.quantize_mx(out=codes[:].bitcast(fmt), scales=scales[:], in_=grouped[:])
             return codes, scales
+
+        def quantize_pilots(i):
+            pilot_mx[i] = quantize(pilot_grouped[i], work, "pilot", E4M3)
+
+        def quantize_clean(i, grouped):
+            clean_mx[i] = quantize(grouped, keep, "clean_mx%d" % i, E5M2)
 
         def make_shrink(i, cols):
             if i not in shrink:
                 shrink[i] = work.tile([P, L], F32, name="shrink", tag="shrink", bufs=2)
-            nc.scalar.activation(out=shrink[i][:, cols], in_=ln_pdp[:, cols], func=ACT.Sigmoid, bias=neg_ln_noise[:, i:i + 1])
+            nc.scalar.activation(out=shrink[i][:, cols], in_=ln_pdp[:, cols], func=ACT.Sigmoid,
+                                 bias=neg_ln_noise[:, i:i + 1])
 
         def taps_matmul(i, h):
             bank = next_bank()
             codes, scales = pilot_mx[i]
             for g in range(PASSES):
-                nc.tensor.matmul_mx(out=bank[:], lhsT=codes[:, g * P:(g + 1) * P].bitcast(E4M3), lhsT_scale=scales[:, g * P:(g + 1) * P],
+                nc.tensor.matmul_mx(out=bank[:], lhsT=codes[:, g * P:(g + 1) * P].bitcast(E4M3),
+                                    lhsT_scale=scales[:, g * P:(g + 1) * P],
                                     rhs=w_words[:, g, 2 * h * BANK:2 * (h + 1) * BANK].bitcast(E2M1),
-                                    rhs_scale=w_scales[:, g, h * BANK:(h + 1) * BANK], start=(g == 0), stop=(g == PASSES - 1))
+                                    rhs_scale=w_scales[:, g, h * BANK:(h + 1) * BANK],
+                                    start=(g == 0), stop=(g == PASSES - 1))
             return bank
 
         def shrink_taps(i, h, bank):
@@ -180,161 +191,157 @@ def tile_delay_domain_denoising_s9_kernel(tc, pilots, to_taps_words, to_taps_sca
                                     in0=bank[:].rearrange("m (p u e) -> m u p e", u=2, e=2),
                                     in1=shrink[i][:, cols].rearrange("m (u p e) -> m u p e", u=2, e=2), op=ALU.mult)
 
-        half = BANK // 2
-
-        def interleave(engine, g, s, first, count):
+        def interleave(copy, g, s, first, count):
             if (g, s) not in sub_grouped:
-                sub_grouped[g, s] = work.tile([P, BANK * PACK], BF16, name="sub_grouped", tag="sub_grouped", bufs=4, align_bytes=64)
+                sub_grouped[g, s] = work.tile([P, BANK * PACK], BF16, name="sub_grouped", tag="sub_grouped", bufs=4,
+                                              align_bytes=64)
             dst = sub_grouped[g, s][:, first * PACK:(first + count) * PACK]
-            copy_on(engine, dst.rearrange("p (c i t) -> p c t i", i=4, t=PACK),
-                    sub_raw[g, s][:, :, first:first + count].rearrange("p t (c i) -> p c t i", i=4))
+            copy(out=dst.rearrange("p (c j t) -> p c t j", j=4, t=PACK),
+                 in_=sub_raw[g, s][:, :, first:first + count].rearrange("p t (c j) -> p c t j", j=4))
 
         def quantize_sub(g, s):
-            name = "sub_mx%d_%d" % (g, s)
-            sub_mx[g, s] = quantize(sub_grouped[g, s], keep, name, name, E4M3)
+            sub_mx[g, s] = quantize(sub_grouped[g, s], keep, "sub_mx%d_%d" % (g, s), E4M3)
 
-        def interleave_half(g, s, h):
-            grouped = work.tile([P, half * PACK], BF16, name="half_grouped", tag="half_grouped", bufs=1, align_bytes=64)
+        gpsimd_halves = [(g, s, h) for g, s in ((1, 0), (0, 1), (0, 2), (1, 2), (0, 4)) for h in range(2)]
+        halves_started = []
+
+        def start_half():
+            g, s, h = gpsimd_halves[len(halves_started)]
+            grouped = work.tile([P, HALF * PACK], BF16, name="half_grouped", tag="half_grouped", bufs=1, align_bytes=64)
             nc.gpsimd.tensor_scalar(out=grouped[:].rearrange("p (c t) -> p c t", t=PACK),
-                                    in0=sub_raw[g, s][:, :, h * half:(h + 1) * half].rearrange("p t c -> p c t"),
+                                    in0=sub_raw[g, s][:, :, h * HALF:(h + 1) * HALF].rearrange("p t c -> p c t"),
                                     scalar1=1.0, scalar2=0.0, op0=ALU.mult, op1=ALU.add)
-            return g, s, h, grouped
+            halves_started.append((g, s, h, grouped))
 
-        def quantize_half(g, s, h, grouped):
+        def quantize_half():
+            g, s, h, grouped = halves_started[-1]
             if (g, s) not in sub_mx:
                 name = "sub_mx%d_%d" % (g, s)
                 sub_mx[g, s] = (keep.tile([P, BANK], U32, name=name + "_codes", align_bytes=64),
                                 keep.tile([P, BANK], U8, name=name + "_scales", align_bytes=64))
             codes, scales = sub_mx[g, s]
-            cols = slice(h * half, (h + 1) * half)
+            cols = slice(h * HALF, (h + 1) * HALF)
             nc.vector.quantize_mx(out=codes[:, cols].bitcast(E4M3), scales=scales[:, cols], in_=grouped[:])
 
         def out_matmul(i, s):
             bank = next_bank()
             codes, scales = clean_mx[i]
             for g in range(PASSES):
-                nc.tensor.matmul_mx(out=bank[:], lhsT=codes[:, g * P:(g + 1) * P].bitcast(E5M2), lhsT_scale=scales[:, g * P:(g + 1) * P],
+                nc.tensor.matmul_mx(out=bank[:], lhsT=codes[:, g * P:(g + 1) * P].bitcast(E5M2),
+                                    lhsT_scale=scales[:, g * P:(g + 1) * P],
                                     rhs=sub_mx[g, s][0][:].bitcast(E4M3), rhs_scale=sub_mx[g, s][1][:],
                                     start=(g == 0), stop=(g == PASSES - 1))
             return bank
 
-        def out_job(i, first, count, shared=()):
+        def out_job(i, first, count, shared):
             banks = [out_matmul(i, first + j) for j in range(count)]
             result = work.tile([P, 2 * BANK], F32, name="result", tag="result", bufs=9)
             for j, bank in enumerate(banks):
                 s = first + j
                 dst = result[:, j * BANK:(j + 1) * BANK]
                 factor = gain[s // 2][:, (s % 2) * BANK:(s % 2 + 1) * BANK]
-                if j in shared:
+                if shared and j == 0:
                     nc.scalar.copy(out=dst, in_=bank[:])
                     nc.gpsimd.tensor_tensor(out=dst, in0=dst, in1=factor, op=ALU.mult)
                 else:
                     nc.vector.tensor_tensor(out=dst, in0=bank[:], in1=factor, op=ALU.mult)
             nc.sync.dma_start(out=out_rows[:, i, first * BANK:(first + count) * BANK], in_=result[:, 0:count * BANK])
 
-        first_bank = turn(pilot_raw[0].bitcast(F32), True)
-        ln_banks = [spread(ln_cols[:, 4 * g:4 * g + 4]) for g in range(PASSES)]
-        pilot_bank = turn(pilot_raw[1].bitcast(F32), True)
-        first_grouped = gather_words("vector", first_bank, "pilot_grouped")
-        pilot_mx[0] = quantize(first_grouped, work, "pilot", "pilot", E4M3)
-        for g, engine in enumerate(("vector", "scalar")):
-            copy_on(engine, ln_pdp[:, g * BANK:(g + 1) * BANK].rearrange("q (u p e) -> q u p e", u=2, e=2),
-                    ln_banks[g][:].rearrange("q (u e p) -> q u p e", u=2, e=2))
+        first_bank = turn_pilots(0)
+        ln_banks = [spread(ln_cols[:, PACK * g:PACK * (g + 1)]) for g in range(PASSES)]
+        pilot_banks = {1: turn_pilots(1)}
+        pilot_grouped[0] = group_pairs(on_vector, first_bank, "pilot_grouped")
+        quantize_pilots(0)
+        for g in range(PASSES):
+            nc.vector.tensor_copy(out=ln_pdp[:, g * BANK:(g + 1) * BANK].rearrange("q (u p e) -> q u p e", u=2, e=2),
+                                  in_=ln_banks[g][:].rearrange("q (u e p) -> q u p e", u=2, e=2))
         for g in range(PASSES):
             make_shrink(0, slice(g * BANK, (g + 1) * BANK))
-        interleave("vector", 0, 0, 0, BANK)
-
-        quarter = BANK // 4
-        gain_steps = (1,)
-        halves = [(g, s, h) for g, s in ((1, 0), (0, 1), (0, 2), (1, 2), (0, 4)) for h in range(2)]
-        pilot_banks = {1: pilot_bank}
-        pilot_grouped = {}
-
-        def quantize_pilots(i):
-            pilot_mx[i] = quantize(pilot_grouped[i], work, "pilot", "pilot", E4M3)
-
-        def quantize_clean(i, grouped):
-            name = "clean_mx%d" % i
-            clean_mx[i] = quantize(grouped, keep, name, name, E5M2)
+        interleave(on_vector, 0, 0, 0, BANK)
 
         for step in range(TILES):
-            ahead, behind = step + 1, step - 2
             for i in sorted(pilot_banks):
-                pilot_grouped[i] = gather_words("scalar", pilot_banks[i], "pilot_grouped")
-            pilot_banks = {}
-            if behind >= 0:
-                clean_grouped = gather_words("scalar", clean_bank, "clean_grouped")
-            if step in (3, 4):
-                interleave("scalar", 1, 1, (step - 2) * quarter, (step - 2) * quarter)
-            if ahead < TILES:
-                make_shrink(ahead, slice(0, L))
+                pilot_grouped[i] = group_pairs(on_scalar, pilot_banks[i], "pilot_grouped")
+            if step >= 2:
+                clean_grouped = group_pairs(on_scalar, clean_bank, "clean_grouped")
+            if step == 3:
+                interleave(on_scalar, 1, 1, QUARTER, QUARTER)
+            if step == 4:
+                interleave(on_scalar, 1, 1, HALF, HALF)
+            if step + 1 < TILES:
+                make_shrink(step + 1, slice(0, L))
             if step == 2:
-                interleave("scalar", 1, 1, 0, quarter)
+                interleave(on_scalar, 1, 1, 0, QUARTER)
             if step in (5, 6):
-                interleave("scalar", 0, 3, (step - 5) * half, half)
+                interleave(on_scalar, 0, 3, (step - 5) * HALF, HALF)
             if step == 6:
-                interleave("scalar", 1, 3, 0, half)
-            if step < TILES:
-                taps = [taps_matmul(step, h) for h in range(2)]
-                clean[step] = work.tile([P, L], BF16, name="clean", tag="clean")
-                shrink_taps(step, 0, taps[0])
-                if step < 2:
-                    quantize_pilots(step + 1)
-                if step == 0:
-                    quantize_sub(0, 0)
-                shrink_taps(step, 1, taps[1])
-            if step == 2:
-                copy_gain("vector", 0, gain_bank)
-            if 3 <= step < TILES:
-                out_job(step - 3, 0, 1 if step < 6 else 2)
-            if 2 < step + 2 < TILES:
+                interleave(on_scalar, 1, 3, 0, HALF)
+
+            taps = [taps_matmul(step, h) for h in range(2)]
+            clean[step] = work.tile([P, L], BF16, name="clean", tag="clean")
+            shrink_taps(step, 0, taps[0])
+            if step < 2:
+                quantize_pilots(step + 1)
+            if step == 0:
+                quantize_sub(0, 0)
+            shrink_taps(step, 1, taps[1])
+            if step + 1 == OUT_LAG:
+                copy_gain(on_vector, 0, gain_bank)
+            if step >= OUT_LAG:
+                out_job(step - OUT_LAG, 0, 2 if step >= FIRST_WIDE_STEP else 1, False)
+
+            if 1 <= step < TILES - 2:
                 quantize_pilots(step + 2)
-            if behind >= 0:
-                quantize_clean(behind, clean_grouped)
+            if step >= 2:
+                quantize_clean(step - 2, clean_grouped)
             if step == 4:
                 quantize_sub(1, 1)
-            if step == 7:
+            if step == TILES - 1:
                 quantize_sub(0, 3)
-            if 1 <= step < TILES - 1:
-                quantize_half(*pending)
-            if step < TILES - 1:
-                pending = interleave_half(*halves[step])
-            for i in range(2 if step == 0 else step + 3, min(step + 4, TILES)):
-                pilot_banks[i] = turn(pilot_raw[i].bitcast(F32), True)
-            if 1 <= step <= TILES:
-                clean_bank = turn(clean[step - 1][:].bitcast(F32), False)
-            if step in gain_steps:
-                gain_bank = spread(gain_cols[:, gain_steps.index(step), :].bitcast(F32))
+            else:
+                if step >= 1:
+                    quantize_half()
+                start_half()
 
-        last_bank = turn(clean[TILES - 1][:].bitcast(F32), False)
-        gain_bank = spread(gain_cols[:, 1, :].bitcast(F32))
-        last_grouped = [gather_words("scalar", bank, "clean_grouped") for bank in (clean_bank, last_bank)]
+            pilot_banks = {i: turn_pilots(i) for i in range(2 if step == 0 else step + 3, min(step + 4, TILES))}
+            if step >= 1:
+                clean_bank = turn_clean(step - 1)
+            if step + 2 == OUT_LAG:
+                gain_bank = spread_gain(0)
+
+        last_bank = turn_clean(TILES - 1)
+        gain_bank = spread_gain(1)
+        last_grouped = [group_pairs(on_scalar, bank, "clean_grouped") for bank in (clean_bank, last_bank)]
         quantize_clean(TILES - 2, last_grouped[0])
         quantize_clean(TILES - 1, last_grouped[1])
-        quantize_half(*pending)
-        pending = interleave_half(*halves[7])
-        interleave("scalar", 1, 3, half, half)
-        copy_gain("scalar", 1, gain_bank)
-        interleave("scalar", 1, 4, 0, BANK)
-        for i in range(3):
-            out_job(i, 1, 1)
+        quantize_half()
+        start_half()
+        interleave(on_scalar, 1, 3, HALF, HALF)
+        copy_gain(on_scalar, 1, gain_bank)
+        interleave(on_scalar, 1, 4, 0, BANK)
+
+        for i in range(FIRST_WIDE_STEP - OUT_LAG):
+            out_job(i, 1, 1, False)
         quantize_sub(1, 3)
-        quantize_half(*pending)
-        pending = interleave_half(*halves[8])
-        pairs = [(i, 0) for i in range(5, TILES)] + [(i, first) for first in (2, 4) for i in range(TILES)]
-        for n, (i, first) in enumerate(pairs[:-1]):
-            out_job(i, first, 2, (0,) if n % 3 == 2 and n < LAST else ())
-            if n in (2, 5):
-                interleave("scalar", n // 3, 5, 0, BANK)
-            if n == 2:
-                quantize_sub(1, 4)
-                quantize_half(*pending)
-                pending = interleave_half(*halves[9])
-            if n == 5:
-                quantize_sub(0, 5)
-                quantize_half(*pending)
-            if n == QN:
+        quantize_half()
+        start_half()
+
+        wide_jobs = [(i, 0) for i in range(TILES - OUT_LAG, TILES)] + [(i, first) for first in (2, 4) for i in range(TILES)]
+        for n, (i, first) in enumerate(wide_jobs[:-1]):
+            round_index, place = divmod(n, SHARE_EVERY)
+            round_ends = place == SHARE_EVERY - 1
+            out_job(i, first, 2, round_ends and n < SHARE_UNTIL)
+            if round_ends and round_index < PASSES:
+                interleave(on_scalar, round_index, 5, 0, BANK)
+                if round_index == 0:
+                    quantize_sub(1, 4)
+                    quantize_half()
+                    start_half()
+                else:
+                    quantize_sub(0, 5)
+                    quantize_half()
+            if n == LAST_UNIT_AFTER:
                 quantize_sub(1, 5)
-                copy_gain("scalar", 2, spread(gain_cols[:, 2, :].bitcast(F32)))
-        out_job(TILES - 1, 4, 1)
-        out_job(TILES - 1, 5, 1)
+                copy_gain(on_scalar, 2, spread_gain(2))
+        out_job(TILES - 1, 4, 1, False)
+        out_job(TILES - 1, 5, 1, False)

from contextlib import ExitStack

import concourse.mybir as mybir
from concourse.masks import make_identity

M, K, L, N = 1024, 1024, 1024, 3072
FLOPS = 2 * M * K * L + 2 * M * L * N

F32 = mybir.dt.float32
BF16 = mybir.dt.bfloat16
I32 = mybir.dt.int32
U32 = mybir.dt.uint32
U8 = mybir.dt.uint8
E4M3 = mybir.dt.float8_e4m3fn_x4
E5M2 = mybir.dt.float8_e5m2_x4
E2M1 = mybir.dt.float4_e2m1fn_x4
ALU = mybir.AluOpType
ACT = mybir.ActivationFunctionType

P = 128
PACK = 4
PASSES = 2
TILES = M // P
BANK = 512
BANKS = 8
HALF = BANK // 2
QUARTER = BANK // 4
LN_EDGE = 2.0 ** 64

OUT_LAG = 3
FIRST_WIDE_STEP = 6
SHARE_EVERY = 3
SHARE_UNTIL = 15
LAST_UNIT_AFTER = 7


def tile_delay_domain_denoising_s9_kernel(tc, pilots, to_taps_words, to_taps_scales, pdp, noise, to_sub,
                                                     front_end, out):
    nc = tc.nc
    pilot_rows = pilots.rearrange("(p i) k -> p i k", i=TILES)
    out_rows = out.rearrange("(p i) n -> p i n", i=TILES)
    sub_rows = to_sub.rearrange("(g p t) n -> g p t n", g=PASSES, t=PACK)

    with ExitStack() as ctx:
        keep = ctx.enter_context(tc.tile_pool(name="keep", bufs=1))
        work = ctx.enter_context(tc.tile_pool(name="work", bufs=3))
        psum = ctx.enter_context(tc.psum_pool(name="psum", bufs=1))
        ctx.enter_context(tc.manual_schedule())

        banks_taken = []

        def next_bank():
            tag = "bank%d" % (len(banks_taken) % BANKS)
            banks_taken.append(tag)
            return psum.tile([P, BANK], F32, name=tag, tag=tag)

        w_scales = keep.tile([P, PASSES, L], U8, name="w_scales", align_bytes=64)
        nc.vector.memset(w_scales[:].rearrange("p g n -> p (g n)").bitcast(I32), 0)
        ident = keep.tile([P, P], F32, name="ident")
        make_identity(nc, ident[:])

        powers = keep.tile([P, 2, 16], BF16, name="powers")
        nc.sync.dma_start(out=powers[:, 0, 0:8].rearrange("p (g t) -> p g t", g=PASSES),
                          in_=pdp.rearrange("(g p t) -> p g t", g=PASSES, t=PACK))
        nc.sync.dma_start(out=powers[:, 1, 0:8], in_=noise.rearrange("(p i) -> p i", i=TILES))

        pilot_raw = {}

        def load_pilots(first, count):
            raw = keep.tile([P, count, K], BF16, name="pilots%d" % first)
            nc.sync.dma_start(out=raw[:], in_=pilot_rows[:, first:first + count, :])
            for i in range(count):
                pilot_raw[first + i] = raw[:, i, :]

        sub_raw = {}

        def load_sub(g, first, count):
            raw = keep.tile([P, PACK, count * BANK], BF16, name="sub%d_%d" % (g, first))
            nc.sync.dma_start(out=raw[:], in_=sub_rows[g][:, :, first * BANK:(first + count) * BANK])
            for s in range(count):
                sub_raw[g, first + s] = raw[:, :, s * BANK:(s + 1) * BANK]

        load_pilots(0, 1)
        scale_rows = to_taps_scales.rearrange("g (q r) n -> r q g n", r=4)
        for r in range(4):
            nc.sync.dma_start(out=w_scales[r:P:32, :, :].bitcast(I32), in_=scale_rows[r].bitcast(I32))
        w_words = keep.tile([P, PASSES, 2 * L], U8, name="w_words", align_bytes=64)
        nc.sync.dma_start(out=w_words[:].bitcast(I32), in_=to_taps_words.rearrange("g p n -> p g n").bitcast(I32))
        load_pilots(1, 1)
        load_sub(0, 0, 1)
        load_pilots(2, 2)
        load_sub(1, 0, 1)
        load_pilots(4, 2)
        gain_cols = keep.tile([P, 3, 8], BF16, name="gain_cols")
        nc.sync.dma_start(out=gain_cols[:], in_=front_end.rearrange("(c p e) -> p c e", p=P, e=8))
        load_sub(0, 1, 1)
        load_sub(1, 1, 1)
        load_pilots(6, 2)
        for first in (2, 4):
            for g in range(PASSES):
                load_sub(g, first, 2)

        factors = keep.tile([P, 3, 16], F32, name="factors")
        splits = ((1.0 / LN_EDGE, LN_EDGE, ALU.max, ALU.min), (LN_EDGE, 1.0 / LN_EDGE, ALU.max, ALU.mult),
                  (1.0 / LN_EDGE, LN_EDGE, ALU.min, ALU.mult))
        for f, (first_scalar, second_scalar, first_op, second_op) in enumerate(splits):
            nc.vector.tensor_scalar(out=factors[:, f, :].rearrange("p (a j) -> p a j", a=2), in0=powers[:, :, 0:8],
                                    scalar1=first_scalar, scalar2=second_scalar, op0=first_op, op1=second_op)
        ln_factors = keep.tile([P, 3, 16], F32, name="ln_factors")
        nc.scalar.activation(out=ln_factors[:], in_=factors[:], func=ACT.Ln)
        ln_cols = keep.tile([P, 16], F32, name="ln_cols")
        nc.vector.tensor_reduce(out=ln_cols[:], in_=ln_factors[:].rearrange("p f j -> p j f"),
                                axis=mybir.AxisListType.X, op=ALU.add)
        neg_ln_noise = keep.tile([P, TILES], F32, name="neg_ln_noise")
        nc.vector.tensor_scalar(out=neg_ln_noise[:], in0=ln_cols[:, 8:16], scalar1=-1.0, scalar2=None, op0=ALU.mult)

        on_scalar, on_vector = nc.scalar.copy, nc.vector.tensor_copy

        def spread(cols):
            bank = next_bank()
            for j in range(4):
                nc.tensor.transpose(bank[:, j * P:(j + 1) * P], cols[:, j:j + 1].to_broadcast([P, P]), ident[:])
            return bank

        ln_pdp = keep.tile([P, L], F32, name="ln_pdp")
        gain = [keep.tile([P, 2 * BANK], BF16, name="gain%d" % c) for c in range(3)]

        def spread_gain(c):
            return spread(gain_cols[:, c, :].bitcast(F32))

        def copy_gain(copy, c, bank):
            copy(out=gain[c][:].bitcast(F32).rearrange("q (p j) -> q p j", j=4),
                 in_=bank[:].rearrange("q (j p) -> q p j", j=4))

        def turn(pair_columns):
            bank = next_bank()
            for g in range(PASSES):
                for u in range(2):
                    nc.tensor.transpose(bank[:, (2 * g + u) * P:(2 * g + u + 1) * P], pair_columns(g, u), ident[:])
            return bank

        def turn_pilots(i):
            pairs = pilot_raw[i].bitcast(F32)
            return turn(lambda g, u: pairs[:, HALF * g + u:HALF * (g + 1):2])

        def turn_clean(i):
            pairs = clean[i][:].bitcast(F32)
            return turn(lambda g, u: pairs[:, HALF * g + P * u:HALF * g + P * (u + 1)])

        def group_pairs(copy, bank, tag):
            grouped = work.tile([P, PASSES * P * PACK], BF16, name=tag, tag=tag, align_bytes=64)
            copy(out=grouped[:].bitcast(F32).rearrange("p (g m u) -> p g m u", g=PASSES, u=2),
                 in_=bank[:].rearrange("p (g u m) -> p g m u", g=PASSES, u=2))
            return grouped

        pilot_grouped, pilot_mx, shrink, clean, clean_mx, sub_grouped, sub_mx = {}, {}, {}, {}, {}, {}, {}

        def quantize(grouped, pool, name, fmt):
            width = grouped.shape[1] // PACK
            codes = pool.tile([P, width], U32, name=name + "_codes", tag=name + "_codes", align_bytes=64)
            scales = pool.tile([P, width], U8, name=name + "_scales", tag=name + "_scales", align_bytes=64)
            nc.vector.quantize_mx(out=codes[:].bitcast(fmt), scales=scales[:], in_=grouped[:])
            return codes, scales

        def quantize_pilots(i):
            pilot_mx[i] = quantize(pilot_grouped[i], work, "pilot", E4M3)

        def quantize_clean(i, grouped):
            clean_mx[i] = quantize(grouped, keep, "clean_mx%d" % i, E5M2)

        def make_shrink(i, cols):
            if i not in shrink:
                shrink[i] = work.tile([P, L], F32, name="shrink", tag="shrink", bufs=2)
            nc.scalar.activation(out=shrink[i][:, cols], in_=ln_pdp[:, cols], func=ACT.Sigmoid,
                                 bias=neg_ln_noise[:, i:i + 1])

        def taps_matmul(i, h):
            bank = next_bank()
            codes, scales = pilot_mx[i]
            for g in range(PASSES):
                nc.tensor.matmul_mx(out=bank[:], lhsT=codes[:, g * P:(g + 1) * P].bitcast(E4M3),
                                    lhsT_scale=scales[:, g * P:(g + 1) * P],
                                    rhs=w_words[:, g, 2 * h * BANK:2 * (h + 1) * BANK].bitcast(E2M1),
                                    rhs_scale=w_scales[:, g, h * BANK:(h + 1) * BANK],
                                    start=(g == 0), stop=(g == PASSES - 1))
            return bank

        def shrink_taps(i, h, bank):
            cols = slice(h * BANK, (h + 1) * BANK)
            nc.vector.tensor_tensor(out=clean[i][:, cols].rearrange("m (u p e) -> m u p e", u=2, e=2),
                                    in0=bank[:].rearrange("m (p u e) -> m u p e", u=2, e=2),
                                    in1=shrink[i][:, cols].rearrange("m (u p e) -> m u p e", u=2, e=2), op=ALU.mult)

        def interleave(copy, g, s, first, count):
            if (g, s) not in sub_grouped:
                sub_grouped[g, s] = work.tile([P, BANK * PACK], BF16, name="sub_grouped", tag="sub_grouped", bufs=4,
                                              align_bytes=64)
            dst = sub_grouped[g, s][:, first * PACK:(first + count) * PACK]
            copy(out=dst.rearrange("p (c j t) -> p c t j", j=4, t=PACK),
                 in_=sub_raw[g, s][:, :, first:first + count].rearrange("p t (c j) -> p c t j", j=4))

        def quantize_sub(g, s):
            sub_mx[g, s] = quantize(sub_grouped[g, s], keep, "sub_mx%d_%d" % (g, s), E4M3)

        gpsimd_halves = [(g, s, h) for g, s in ((1, 0), (0, 1), (0, 2), (1, 2), (0, 4)) for h in range(2)]
        halves_started = []

        def start_half():
            g, s, h = gpsimd_halves[len(halves_started)]
            grouped = work.tile([P, HALF * PACK], BF16, name="half_grouped", tag="half_grouped", bufs=1, align_bytes=64)
            nc.gpsimd.tensor_scalar(out=grouped[:].rearrange("p (c t) -> p c t", t=PACK),
                                    in0=sub_raw[g, s][:, :, h * HALF:(h + 1) * HALF].rearrange("p t c -> p c t"),
                                    scalar1=1.0, scalar2=0.0, op0=ALU.mult, op1=ALU.add)
            halves_started.append((g, s, h, grouped))

        def quantize_half():
            g, s, h, grouped = halves_started[-1]
            if (g, s) not in sub_mx:
                name = "sub_mx%d_%d" % (g, s)
                sub_mx[g, s] = (keep.tile([P, BANK], U32, name=name + "_codes", align_bytes=64),
                                keep.tile([P, BANK], U8, name=name + "_scales", align_bytes=64))
            codes, scales = sub_mx[g, s]
            cols = slice(h * HALF, (h + 1) * HALF)
            nc.vector.quantize_mx(out=codes[:, cols].bitcast(E4M3), scales=scales[:, cols], in_=grouped[:])

        def out_matmul(i, s):
            bank = next_bank()
            codes, scales = clean_mx[i]
            for g in range(PASSES):
                nc.tensor.matmul_mx(out=bank[:], lhsT=codes[:, g * P:(g + 1) * P].bitcast(E5M2),
                                    lhsT_scale=scales[:, g * P:(g + 1) * P],
                                    rhs=sub_mx[g, s][0][:].bitcast(E4M3), rhs_scale=sub_mx[g, s][1][:],
                                    start=(g == 0), stop=(g == PASSES - 1))
            return bank

        def out_job(i, first, count, shared):
            banks = [out_matmul(i, first + j) for j in range(count)]
            result = work.tile([P, 2 * BANK], F32, name="result", tag="result", bufs=9)
            for j, bank in enumerate(banks):
                s = first + j
                dst = result[:, j * BANK:(j + 1) * BANK]
                factor = gain[s // 2][:, (s % 2) * BANK:(s % 2 + 1) * BANK]
                if shared and j == 0:
                    nc.scalar.copy(out=dst, in_=bank[:])
                    nc.gpsimd.tensor_tensor(out=dst, in0=dst, in1=factor, op=ALU.mult)
                else:
                    nc.vector.tensor_tensor(out=dst, in0=bank[:], in1=factor, op=ALU.mult)
            nc.sync.dma_start(out=out_rows[:, i, first * BANK:(first + count) * BANK], in_=result[:, 0:count * BANK])

        first_bank = turn_pilots(0)
        ln_banks = [spread(ln_cols[:, PACK * g:PACK * (g + 1)]) for g in range(PASSES)]
        pilot_banks = {1: turn_pilots(1)}
        pilot_grouped[0] = group_pairs(on_vector, first_bank, "pilot_grouped")
        quantize_pilots(0)
        for g in range(PASSES):
            nc.vector.tensor_copy(out=ln_pdp[:, g * BANK:(g + 1) * BANK].rearrange("q (u p e) -> q u p e", u=2, e=2),
                                  in_=ln_banks[g][:].rearrange("q (u e p) -> q u p e", u=2, e=2))
        for g in range(PASSES):
            make_shrink(0, slice(g * BANK, (g + 1) * BANK))
        interleave(on_vector, 0, 0, 0, BANK)

        for step in range(TILES):
            for i in sorted(pilot_banks):
                pilot_grouped[i] = group_pairs(on_scalar, pilot_banks[i], "pilot_grouped")
            if step >= 2:
                clean_grouped = group_pairs(on_scalar, clean_bank, "clean_grouped")
            if step == 3:
                interleave(on_scalar, 1, 1, QUARTER, QUARTER)
            if step == 4:
                interleave(on_scalar, 1, 1, HALF, HALF)
            if step + 1 < TILES:
                make_shrink(step + 1, slice(0, L))
            if step == 2:
                interleave(on_scalar, 1, 1, 0, QUARTER)
            if step in (5, 6):
                interleave(on_scalar, 0, 3, (step - 5) * HALF, HALF)
            if step == 6:
                interleave(on_scalar, 1, 3, 0, HALF)

            taps = [taps_matmul(step, h) for h in range(2)]
            clean[step] = work.tile([P, L], BF16, name="clean", tag="clean")
            shrink_taps(step, 0, taps[0])
            if step < 2:
                quantize_pilots(step + 1)
            if step == 0:
                quantize_sub(0, 0)
            shrink_taps(step, 1, taps[1])
            if step + 1 == OUT_LAG:
                copy_gain(on_vector, 0, gain_bank)
            if step >= OUT_LAG:
                out_job(step - OUT_LAG, 0, 2 if step >= FIRST_WIDE_STEP else 1, False)

            if 1 <= step < TILES - 2:
                quantize_pilots(step + 2)
            if step >= 2:
                quantize_clean(step - 2, clean_grouped)
            if step == 4:
                quantize_sub(1, 1)
            if step == TILES - 1:
                quantize_sub(0, 3)
            else:
                if step >= 1:
                    quantize_half()
                start_half()

            pilot_banks = {i: turn_pilots(i) for i in range(2 if step == 0 else step + 3, min(step + 4, TILES))}
            if step >= 1:
                clean_bank = turn_clean(step - 1)
            if step + 2 == OUT_LAG:
                gain_bank = spread_gain(0)

        last_bank = turn_clean(TILES - 1)
        gain_bank = spread_gain(1)
        last_grouped = [group_pairs(on_scalar, bank, "clean_grouped") for bank in (clean_bank, last_bank)]
        quantize_clean(TILES - 2, last_grouped[0])
        quantize_clean(TILES - 1, last_grouped[1])
        quantize_half()
        start_half()
        interleave(on_scalar, 1, 3, HALF, HALF)
        copy_gain(on_scalar, 1, gain_bank)
        interleave(on_scalar, 1, 4, 0, BANK)

        for i in range(FIRST_WIDE_STEP - OUT_LAG):
            out_job(i, 1, 1, False)
        quantize_sub(1, 3)
        quantize_half()
        start_half()

        wide_jobs = [(i, 0) for i in range(TILES - OUT_LAG, TILES)] + [(i, first) for first in (2, 4) for i in range(TILES)]
        for n, (i, first) in enumerate(wide_jobs[:-1]):
            round_index, place = divmod(n, SHARE_EVERY)
            round_ends = place == SHARE_EVERY - 1
            out_job(i, first, 2, round_ends and n < SHARE_UNTIL)
            if round_ends and round_index < PASSES:
                interleave(on_scalar, round_index, 5, 0, BANK)
                if round_index == 0:
                    quantize_sub(1, 4)
                    quantize_half()
                    start_half()
                else:
                    quantize_sub(0, 5)
                    quantize_half()
            if n == LAST_UNIT_AFTER:
                quantize_sub(1, 5)
                copy_gain(on_scalar, 2, spread_gain(2))
        out_job(TILES - 1, 4, 1, False)
        out_job(TILES - 1, 5, 1, False)
